import numpy as np
import ml_dtypes


def mxq(x, axis, fmt="e4m3"):
    dtype, down = {"e4m3": (ml_dtypes.float8_e4m3fn, 7), "e5m2": (ml_dtypes.float8_e5m2, 14)}[fmt]
    v = np.moveaxis(np.asarray(x, np.float32).astype(ml_dtypes.bfloat16).astype(np.float64), axis, -1)
    blocks = v.reshape(v.shape[:-1] + (-1, 32))
    amax = np.abs(blocks).max(-1, keepdims=True)
    byte = np.maximum(np.where(amax > 0, np.frexp(amax)[1] - 1 + 127, 0) - down, 1)
    scale = np.exp2(byte - 127.0)
    codes = (blocks / scale).astype(np.float32).astype(dtype).astype(np.float64)
    return np.moveaxis((codes * scale).reshape(v.shape), -1, axis)


WIDE = False


def mx_kscale(k):
    if not WIDE:
        return np.ones(k)
    levels = np.array([10, -10, 5, -5, 0])
    if k % 512:
        return np.exp2(np.random.permutation(np.resize(levels, k // 32))).repeat(32)
    a = np.empty((k // 512, 16))
    for p in range(k // 512):
        a[p, :8] = np.random.permutation(np.resize(levels, 8))
        for g in range(8):
            far = levels[np.abs(levels - a[p, g]) >= 10]
            a[p, g + 8] = far[np.random.randint(len(far))]
    return np.exp2(a.ravel()).repeat(32)


def f64(x):
    return np.asarray(x).astype(np.float64)


def striped(idx):
    return np.tile(idx.reshape(-1, 16).T, (8, 1)).astype(np.uint16)


def unstriped(offs):
    return offs[:16].T.reshape(-1).astype(np.int64)


E2M1 = np.array([0.0, 0.5, 1.0, 1.5, 2.0, 3.0, 4.0, 6.0, -0.0, -0.5, -1.0, -1.5, -2.0, -3.0, -4.0, -6.0])


def pack_weight(w, fmt):
    k, n = w.shape
    w = f64(np.asarray(w, np.float32).astype(ml_dtypes.bfloat16)).reshape(k // 32, 32, n)
    amax = np.abs(w).max(1)
    if fmt == "e4m3":
        byte = np.frexp(amax)[1] - 1 + 127 - 7
    else:
        mant, ex = np.frexp(amax / 6.0)
        byte = np.where(mant > 0.5, ex, ex - 1) + 127
    byte = np.clip(np.where(amax > 0, byte, 1), 1, 254)
    scaled = (w * np.exp2(127.0 - byte)[:, None, :]).reshape(k, n).astype(np.float32)
    by_word = np.ascontiguousarray(scaled.reshape(k // 512, 128, 4, n).transpose(0, 1, 3, 2))
    if fmt == "e4m3":
        words = by_word.astype(ml_dtypes.float8_e4m3fn).view(np.uint8)
    else:
        c = by_word.astype(ml_dtypes.float4_e2m1fn).view(np.uint8) & 0xF
        words = (c[..., 0::2] | (c[..., 1::2] << 4)).reshape(k // 512, 128, 2 * n)
    return np.ascontiguousarray(words), np.ascontiguousarray(byte.astype(np.uint8).reshape(k // 512, 16, n))


def unpack_weight(words, scales, fmt):
    g, _, n = scales.shape
    words = np.ascontiguousarray(words).reshape(g, 128, n, -1)
    if fmt == "e4m3":
        vals = words.view(ml_dtypes.float8_e4m3fn).astype(np.float64)
    else:
        nib = np.empty((g, 128, n, 4), np.uint8)
        nib[..., 0::2] = words & 0xF
        nib[..., 1::2] = words >> 4
        vals = E2M1[nib]
    vals = vals * np.repeat(np.exp2(scales.astype(np.float64) - 127.0), 8, axis=1)[..., None]
    return vals.transpose(0, 1, 3, 2).reshape(g * 512, n)


def d_silu(v):
    s = 1.0 / (1.0 + np.exp(-np.maximum(v, -700.0)))
    return s * (1.0 + v * (1.0 - s))


K, T, E, C, H, N = 128, 768, 12, 256, 1024, 512
TOP = 4


def by_expert(wq, xq):
    return np.concatenate([wq[e].T @ xq[:, e * C:(e + 1) * C] for e in range(E)], axis=1)


def setup_inputs():
    n = np.random.standard_normal
    s = mx_kscale(N)[:, None]
    u = mx_kscale(H)
    deal = np.repeat(np.arange(E), C).reshape(TOP, T)[:, np.random.permutation(T)]
    deal = np.take_along_axis(deal, np.argsort(np.random.rand(TOP, T), axis=0), axis=0)
    for _ in range(8):
        s_, t_ = np.random.permutation(T).reshape(2, -1); r = np.random.randint(TOP, size=T // 2); x, y = deal[r, s_].copy(), deal[r, t_].copy()
        ok = ~((deal[:, s_] == y).any(0) | (deal[:, t_] == x).any(0)); deal[r[ok], s_[ok]] = y[ok]; deal[r[ok], t_[ok]] = x[ok]
    order = np.lexsort((np.random.rand(TOP * T), deal.reshape(-1)))
    slot_token = order % T; pos = np.empty(TOP * T, np.int64); pos[order] = np.arange(TOP * T); pos = pos.reshape(TOP, T)
    g = np.random.uniform(0.5, 1.5, (TOP, T)); g = g / g.sum(0)
    w_slot = np.empty(E * C)
    for r in range(TOP): w_slot[pos[r]] = g[r]
    dy = pack_weight(n((N, T)) * s, "e4m3")
    return {
        "dy_words": dy[0],
        "dy_scales": dy[1],
        "a": n((H, E * C)).astype(np.float32),
        "w2": (n((E, N, H)) / np.sqrt(N) / s[None] * u[None, None, :]).astype(np.float32),
        "w1": (n((E, H, K)) / np.sqrt(H) / u[None, :, None]).astype(np.float32),
        "gate": np.tile(w_slot, (H, 1)).astype(np.float32),
        "offs": striped(slot_token),
        "pos1": striped(pos[0]),
        "pos2": striped(pos[1]),
        "pos3": striped(pos[2]),
        "pos4": striped(pos[3]),
    }


def reference(dy_words, dy_scales, a, w2, w1, gate, offs, pos1, pos2, pos3, pos4):
    idx = unstriped(offs)
    gq = unpack_weight(dy_words, dy_scales, "e4m3")[:, idx]
    dh = f64(gate) * by_expert(mxq(f64(w2), 1, "e4m3"), gq)
    da = dh * d_silu(f64(a))
    dx = by_expert(mxq(f64(w1), 1, "e4m3"), mxq(da, 0, "e4m3"))
    return dx[:, unstriped(pos1)] + dx[:, unstriped(pos2)] + dx[:, unstriped(pos3)] + dx[:, unstriped(pos4)]

@@ -1,0 +1,301 @@
+from contextlib import ExitStack
+
+import concourse.mybir as mybir
+from concourse.masks import make_identity
+
+K, T, E, C, H, N = 128, 768, 12, 256, 1024, 512
+S = E * C
+FLOPS = 2 * S * H * (N + K)
+BYTES = 4 * (E * N * H + E * H * K + H * S + S + K * T) + 128 * T * 4 + 16 * T + 128 * 2 * (S + 4 * T) // 16
+
+F32 = mybir.dt.float32
+BF16 = mybir.dt.bfloat16
+I32 = mybir.dt.int32
+U32 = mybir.dt.uint32
+U16 = mybir.dt.uint16
+U8 = mybir.dt.uint8
+FP8X4 = mybir.dt.float8_e4m3fn_x4
+ALU = mybir.AluOpType
+ACT = mybir.ActivationFunctionType
+
+P = 128
+HALF = 512
+TILES = S // P
+UNITS = 2 * TILES
+GATHER = 512
+V_COLS = 320
+A_CHUNKS = [(0, 1), (1, 2), (2, 4), (4, 6), (6, 8), (8, 10), (10, 12)]
+
+
+def tile_moe_bdx_mlp_silu_kernel(
+    tc, dy_words, dy_scales, a, w2, w1, gate, offs, pos1, pos2, pos3, pos4, out
+):
+    nc = tc.nc
+    with ExitStack() as ctx:
+        keep = ctx.enter_context(tc.tile_pool(name="keep", bufs=1))
+        load = ctx.enter_context(tc.tile_pool(name="load", bufs=3))
+        work = ctx.enter_context(tc.tile_pool(name="work", bufs=3))
+        psum = ctx.enter_context(tc.psum_pool(name="psum", bufs=2))
+
+        offs_sb = keep.tile([P, S // 16], U16, name="offs_sb")
+        nc.sync.dma_start(offs_sb[:], offs)
+        words = keep.tile([P, T], I32, name="words", align_bytes=64)
+        nc.sync.dma_start(words[:], dy_words[0].rearrange("p t d -> p (t d)").bitcast(I32))
+        scales = keep.tile([P, T], U8, name="scales", align_bytes=64)
+        nc.gpsimd.memset(scales[:], 0)
+        for q in range(4):
+            nc.scalar.dma_start(
+                scales[32 * q : 32 * q + 4, :].bitcast(I32), dy_scales[0, 4 * q : 4 * q + 4, :].bitcast(I32)
+            )
+        ident = keep.tile([P, P], F32, name="ident")
+        make_identity(nc, ident[:])
+        ones = keep.tile([P, P], F32, name="ones")
+        nc.vector.memset(ones[:], 1.0)
+
+        a_view = a.rearrange("(b q u) s -> u q b s", q=P, u=2)
+        a_sb, w2_raw, w1_raw = {}, {}, {}
+
+        def load_expert(e):
+            for first, last in A_CHUNKS:
+                if first == e:
+                    for u in range(2):
+                        t = load.tile([P, 4, (last - first) * C], F32, name="a_sb", bufs=6)
+                        nc.sync.dma_start(t[:], a_view[u, :, :, first * C : last * C])
+                        for x in range(first, last):
+                            a_sb[x, u] = (t, (x - first) * C)
+            raw2 = load.tile([P, 4, H], F32, name="w2_raw")
+            src2 = w2[e].rearrange("(p j) h -> p j h", j=4)
+            if e == 0:
+                for g in range(2):
+                    cols = slice(g * HALF, (g + 1) * HALF)
+                    nc.sync.dma_start(raw2[:, :, cols], src2[:, :, cols])
+            else:
+                nc.sync.dma_start(raw2[:], src2)
+            w2_raw[e] = raw2
+            raw1 = load.tile([P, 2, 4 * K], F32, name="w1_raw")
+            nc.sync.dma_start(raw1[:], w1[e].rearrange("(g p j) k -> p g (j k)", g=2, j=4))
+            w1_raw[e] = raw1
+
+        load_expert(0)
+        gate_rows = keep.tile([P, P], F32, name="gate_rows")
+        nc.sync.dma_start(gate_rows[:], gate.rearrange("h (t p) -> (h t) p", p=P)[0:P, :])
+        load_expert(1)
+        pos_sb = []
+        for r, pos in enumerate((pos1, pos2, pos3, pos4)):
+            t = keep.tile([P, T // 16], U16, name="pos%d" % r)
+            nc.sync.dma_start(t[:], pos)
+            pos_sb.append(t)
+
+        g_words, g_scales = {}, {}
+
+        def gather_words(c):
+            t = keep.tile([P, GATHER], U32, name="g_words%d" % c, align_bytes=64)
+            cols = slice(c * GATHER // 16, (c + 1) * GATHER // 16)
+            nc.vector.tensor_copy(t[:], words[:].bitcast(U32).indirect(offs_sb[:, cols]))
+            g_words[c] = t
+
+        def gather_scales(c):
+            t = keep.tile([P, GATHER], U8, name="g_scales%d" % c, align_bytes=64)
+            cols = slice(c * GATHER // 16, (c + 1) * GATHER // 16)
+            nc.vector.tensor_copy(t[:], scales[:].indirect(offs_sb[:, cols]))
+            g_scales[c] = t
+
+        w2_bf, w2_mx, w1_bf, w1_mx = {}, {}, {}, {}
+
+        def cast_w2(e, lo, hi, on_vector):
+            g = lo // HALF
+            if (e, g) not in w2_bf:
+                w2_bf[e, g] = work.tile([P, HALF, 4], BF16, name="w2_bf", align_bytes=64)
+            dst = w2_bf[e, g][:, lo - g * HALF : hi - g * HALF, :].rearrange("p (c i) j -> p c j i", i=4)
+            src = w2_raw[e][:, :, lo:hi].rearrange("p j (c i) -> p c j i", i=4)
+            if on_vector:
+                nc.vector.tensor_copy(dst, src)
+            else:
+                nc.scalar.copy(dst, src)
+
+        def quantise(src, width, name, bufs):
+            codes = work.tile([P, width], U32, name=name + "_codes", align_bytes=64, bufs=bufs)
+            plane = work.tile([P, width], U8, name=name + "_plane", align_bytes=64, bufs=bufs)
+            nc.vector.quantize_mx(out=codes[:].bitcast(FP8X4), scales=plane[:], in_=src)
+            return codes, plane
+
+        def quant_w2(e, g):
+            w2_mx[e, g] = quantise(w2_bf[e, g][:].rearrange("p c j -> p (c j)"), HALF, "w2", 4)
+
+        def cast_w1(e, g):
+            if e not in w1_bf:
+                w1_bf[e] = work.tile([P, 2, 4 * K], BF16, name="w1_bf", align_bytes=64, bufs=2)
+            nc.vector.tensor_copy(
+                w1_bf[e][:, g, :].rearrange("p (k u x) -> p k u x", u=2, x=2),
+                w1_raw[e][:, g, :].rearrange("p (x u k) -> p k u x", u=2, x=2),
+            )
+
+        def quant_w1(e):
+            w1_mx[e] = quantise(w1_bf[e][:].rearrange("p g c -> p (g c)"), 2 * K, "w1", 3)
+
+        def prepare(e, k):
+            if k == 0:
+                cast_w2(e, V_COLS, HALF, False)
+                cast_w2(e, 0, V_COLS, True)
+            elif k == 1:
+                cast_w2(e, HALF, HALF + 256, False)
+                quant_w2(e, 0)
+            elif k == 2:
+                cast_w2(e, HALF + 256, H, False)
+                cast_w1(e, 0)
+                cast_w1(e, 1)
+            else:
+                quant_w2(e, 1)
+                quant_w1(e)
+
+        tanh_sb, silu_sb, t1_ps, prod_ps, y_sb, da_sb, da_in = {}, {}, {}, {}, {}, {}, {}
+
+        def a_block(st, u):
+            t, base = a_sb[st // 2, u]
+            lo = base + (st % 2) * P
+            return t[:, :, lo : lo + P]
+
+        def tanh_tile(st):
+            t = work.tile([P, 2, 4, P], F32, name="tanh_sb")
+            for u in range(2):
+                nc.scalar.activation(t[:, u, :, :], a_block(st, u), ACT.Tanh, scale=0.5)
+            tanh_sb[st] = t
+
+        def silu_unit(n):
+            st, g = divmod(n, 2)
+            a_t = psum.tile([P, 4, P], F32, name="a_t")
+            for u in range(2):
+                for b in range(2):
+                    nc.tensor.transpose(a_t[:, 2 * u + b, :], a_block(st, u)[:, 2 * g + b, :], ident[:])
+            r = work.tile([P, HALF], F32, name="silu_sb", bufs=4)
+            nc.scalar.activation(r[:], a_t[:].rearrange("p b q -> p (b q)"), ACT.Silu, scale=-1.0)
+            silu_sb[n] = r
+
+        def one_plus_tanh(n):
+            st, g = divmod(n, 2)
+            t1 = psum.tile([P, 4, P], F32, name="t1")
+            for u in range(2):
+                for b in range(2):
+                    dst = t1[:, 2 * u + b, :]
+                    nc.tensor.matmul(dst, ones[:], ident[:], start=True, stop=False, is_transpose=True)
+                    nc.tensor.matmul(
+                        dst, tanh_sb[st][:, u, 2 * g + b, :], ident[:], start=False, stop=True, is_transpose=True
+                    )
+            t1_ps[n] = t1
+
+        def product(n):
+            st, g = divmod(n, 2)
+            c, lo = divmod(st * P, GATHER)
+            codes, plane = w2_mx[st // 2, g]
+            acc = psum.tile([P, HALF], F32, name="prod")
+            nc.tensor.matmul_mx(
+                out=acc[:],
+                lhsT=g_words[c][:, lo : lo + P].bitcast(FP8X4),
+                lhsT_scale=g_scales[c][:, lo : lo + P],
+                rhs=codes[:].bitcast(FP8X4),
+                rhs_scale=plane[:],
+                start=True,
+                stop=True,
+            )
+            prod_ps[n] = acc
+
+        def derivative(n):
+            y = work.tile([P, HALF], F32, name="y_sb")
+            nc.vector.scalar_tensor_tensor(
+                y[:], silu_sb[n][:], 1.0, t1_ps[n][:].rearrange("p b q -> p (b q)"), ALU.subtract, ALU.mult
+            )
+            y_sb[n] = y
+
+        def make_da(n):
+            st = n // 2
+            da = work.tile([P, HALF], BF16, name="da_sb", bufs=4)
+            nc.vector.scalar_tensor_tensor(
+                da[:].rearrange("p (u m) -> p u m", u=2),
+                prod_ps[n][:].rearrange("p (m u) -> p u m", u=2),
+                gate_col[:, st : st + 1],
+                y_sb[n][:].rearrange("p (u m) -> p u m", u=2),
+                ALU.mult,
+                ALU.mult,
+            )
+            da_sb[n] = da
+
+        def turn_da(st):
+            e, half = divmod(st, 2)
+            if half == 0:
+                da_in[e] = work.tile([P, 2, C, 4], BF16, name="da_in", align_bytes=64, bufs=2)
+            da_t = psum.tile([P, 2, 2, P], F32, name="da_t", bufs=1)
+            for g in range(2):
+                pairs = da_sb[2 * st + g][:].bitcast(F32)
+                for u in range(2):
+                    nc.tensor.transpose(da_t[:, g, u, :], pairs[:, u * P : (u + 1) * P], ident[:])
+            dst = da_in[e][:].rearrange("p g s t -> p g (s t)").bitcast(F32)
+            nc.scalar.copy(
+                dst[:, :, half * 2 * P : (half + 1) * 2 * P].rearrange("p g (s u) -> p g s u", u=2),
+                da_t[:].rearrange("p g u s -> p g s u"),
+            )
+
+        dx_all = keep.tile([P, S], F32, name="dx_all")
+
+        def second_product(e):
+            codes, plane = quantise(da_in[e][:].rearrange("p g s t -> p (g s t)"), 2 * C, "da", 2)
+            w_codes, w_plane = w1_mx[e]
+            acc = psum.tile([P, C], F32, name="dx", bufs=1)
+            for g in range(2):
+                nc.tensor.matmul_mx(
+                    out=acc[:],
+                    lhsT=w_codes[:, g * K : (g + 1) * K].bitcast(FP8X4),
+                    lhsT_scale=w_plane[:, g * K : (g + 1) * K],
+                    rhs=codes[:, g * C : (g + 1) * C].bitcast(FP8X4),
+                    rhs_scale=plane[:, g * C : (g + 1) * C],
+                    start=(g == 0),
+                    stop=(g == 1),
+                )
+            nc.scalar.copy(dx_all[:, e * C : (e + 1) * C], acc[:])
+
+        gather_words(0)
+        gather_scales(0)
+        gate_t = psum.tile([P, P], F32, name="dx", bufs=1)
+        nc.tensor.transpose(gate_t[:], gate_rows[:], ident[:])
+        gate_col = keep.tile([P, TILES], F32, name="gate_col")
+        nc.vector.tensor_scalar_mul(gate_col[:], gate_t[:, 0:TILES], -0.5)
+        tanh_tile(0)
+        for k in range(4):
+            prepare(0, k)
+
+        for n in range(-3, UNITS + 3):
+            if 0 <= n + 1 < UNITS:
+                derivative(n + 1)
+            if 0 <= n < UNITS:
+                make_da(n)
+            if 0 <= n + 1 < UNITS:
+                product(n + 1)
+            if n + 3 < UNITS:
+                silu_unit(n + 3)
+            if 0 <= n + 2 < UNITS:
+                one_plus_tanh(n + 2)
+            if n >= 1 and n % 2 == 1 and n // 2 < TILES:
+                turn_da(n // 2)
+            if n % 2 == 0 and 1 <= (n + 4) // 2 < TILES:
+                tanh_tile((n + 4) // 2)
+            if n >= 5 and n % 4 == 1:
+                second_product(n // 4 - 1)
+            e, k = divmod(n + 1, 4)
+            if 0 <= e and e + 1 < E:
+                if k == 0 and e + 2 < E:
+                    load_expert(e + 2)
+                prepare(e + 1, k)
+                if e % 2 == 1 and k == 0:
+                    gather_words((e + 1) // 2)
+                if e % 2 == 1 and k == 2:
+                    gather_scales((e + 1) // 2)
+
+        picked = [keep.tile([P, T], F32, name="picked%d" % r) for r in range(4)]
+        for r in range(3):
+            nc.vector.tensor_copy(picked[r][:], dx_all[:].indirect(pos_sb[r][:]))
+        nc.vector.tensor_add(picked[0][:], picked[0][:], picked[1][:])
+        nc.vector.tensor_copy(picked[3][:], dx_all[:].indirect(pos_sb[3][:]))
+        nc.vector.tensor_add(picked[0][:], picked[0][:], picked[2][:])
+        for h in range(2):
+            cols = slice(h * T // 2, (h + 1) * T // 2)
+            nc.vector.tensor_add(picked[0][:, cols], picked[0][:, cols], picked[3][:, cols])
+            nc.sync.dma_start(out[:, cols], picked[0][:, cols])

@@ -23,7 +23,7 @@ HALF = 512
 TILES = S // P
 UNITS = 2 * TILES
 GATHER = 512
-V_COLS = 320
+V_COLS = 224
 A_CHUNKS = [(0, 1), (1, 2), (2, 4), (4, 6), (6, 8), (8, 10), (10, 12)]
 
 
@@ -49,13 +49,11 @@ def tile_moe_bdx_mlp_silu_kernel(
             )
         ident = keep.tile([P, P], F32, name="ident")
         make_identity(nc, ident[:])
-        ones = keep.tile([P, P], F32, name="ones")
-        nc.vector.memset(ones[:], 1.0)
 
         a_view = a.rearrange("(b q u) s -> u q b s", q=P, u=2)
         a_sb, w2_raw, w1_raw = {}, {}, {}
 
-        def load_expert(e):
+        def load_a(e):
             for first, last in A_CHUNKS:
                 if first == e:
                     for u in range(2):
@@ -63,14 +61,17 @@ def tile_moe_bdx_mlp_silu_kernel(
                         nc.sync.dma_start(t[:], a_view[u, :, :, first * C : last * C])
                         for x in range(first, last):
                             a_sb[x, u] = (t, (x - first) * C)
+
+        def load_expert(e):
             raw2 = load.tile([P, 4, H], F32, name="w2_raw")
             src2 = w2[e].rearrange("(p j) h -> p j h", j=4)
             if e == 0:
-                for g in range(2):
-                    cols = slice(g * HALF, (g + 1) * HALF)
-                    nc.sync.dma_start(raw2[:, :, cols], src2[:, :, cols])
+                nc.sync.dma_start(raw2[:, :, 0:HALF], src2[:, :, 0:HALF])
+                load_a(e)
+                nc.sync.dma_start(raw2[:, :, HALF:H], src2[:, :, HALF:H])
             else:
                 nc.sync.dma_start(raw2[:], src2)
+                load_a(e)
             w2_raw[e] = raw2
             raw1 = load.tile([P, 2, 4 * K], F32, name="w1_raw")
             nc.sync.dma_start(raw1[:], w1[e].rearrange("(g p j) k -> p g (j k)", g=2, j=4))
@@ -148,40 +149,30 @@ def tile_moe_bdx_mlp_silu_kernel(
                 quant_w2(e, 1)
                 quant_w1(e)
 
-        tanh_sb, silu_sb, t1_ps, prod_ps, y_sb, da_sb, da_in = {}, {}, {}, {}, {}, {}, {}
+        tanh_sb, silu_sb, prod_ps, y_sb, da_sb, da_in = {}, {}, {}, {}, {}, {}
 
         def a_block(st, u):
             t, base = a_sb[st // 2, u]
             lo = base + (st % 2) * P
             return t[:, :, lo : lo + P]
 
-        def tanh_tile(st):
-            t = work.tile([P, 2, 4, P], F32, name="tanh_sb")
-            for u in range(2):
-                nc.scalar.activation(t[:, u, :, :], a_block(st, u), ACT.Tanh, scale=0.5)
-            tanh_sb[st] = t
-
-        def silu_unit(n):
+        def activations(n):
             st, g = divmod(n, 2)
-            a_t = psum.tile([P, 4, P], F32, name="a_t")
+            a_t = psum.tile([P, 4, P], F32, name="a_t", bufs=3)
             for u in range(2):
                 for b in range(2):
                     nc.tensor.transpose(a_t[:, 2 * u + b, :], a_block(st, u)[:, 2 * g + b, :], ident[:])
-            r = work.tile([P, HALF], F32, name="silu_sb", bufs=4)
-            nc.scalar.activation(r[:], a_t[:].rearrange("p b q -> p (b q)"), ACT.Silu, scale=-1.0)
-            silu_sb[n] = r
+            if g == 0:
+                tanh_sb[st] = work.tile([P, H], F32, name="tanh_sb")
+                silu_sb[st] = work.tile([P, H], F32, name="silu_sb")
+            cols = slice(g * HALF, (g + 1) * HALF)
+            flat = a_t[:].rearrange("p b q -> p (b q)")
+            nc.scalar.activation(tanh_sb[st][:, cols], flat, ACT.Tanh, scale=0.5)
+            nc.scalar.activation(silu_sb[st][:, cols], flat, ACT.Silu, scale=-1.0)
 
-        def one_plus_tanh(n):
-            st, g = divmod(n, 2)
-            t1 = psum.tile([P, 4, P], F32, name="t1")
-            for u in range(2):
-                for b in range(2):
-                    dst = t1[:, 2 * u + b, :]
-                    nc.tensor.matmul(dst, ones[:], ident[:], start=True, stop=False, is_transpose=True)
-                    nc.tensor.matmul(
-                        dst, tanh_sb[st][:, u, 2 * g + b, :], ident[:], start=False, stop=True, is_transpose=True
-                    )
-            t1_ps[n] = t1
+        def gated_sigmoid(st):
+            col = gate_col[:, st : st + 1]
+            nc.vector.tensor_scalar(tanh_sb[st][:], tanh_sb[st][:], col, col, ALU.mult, ALU.add)
 
         def product(n):
             st, g = divmod(n, 2)
@@ -199,22 +190,18 @@ def tile_moe_bdx_mlp_silu_kernel(
             )
             prod_ps[n] = acc
 
-        def derivative(n):
-            y = work.tile([P, HALF], F32, name="y_sb")
-            nc.vector.scalar_tensor_tensor(
-                y[:], silu_sb[n][:], 1.0, t1_ps[n][:].rearrange("p b q -> p (b q)"), ALU.subtract, ALU.mult
-            )
-            y_sb[n] = y
+        def derivative(st):
+            y = work.tile([P, H], F32, name="y_sb", bufs=2)
+            nc.vector.scalar_tensor_tensor(y[:], silu_sb[st][:], 1.0, tanh_sb[st][:], ALU.subtract, ALU.mult)
+            y_sb[st] = y
 
         def make_da(n):
-            st = n // 2
+            st, g = divmod(n, 2)
             da = work.tile([P, HALF], BF16, name="da_sb", bufs=4)
-            nc.vector.scalar_tensor_tensor(
+            nc.vector.tensor_tensor(
                 da[:].rearrange("p (u m) -> p u m", u=2),
                 prod_ps[n][:].rearrange("p (m u) -> p u m", u=2),
-                gate_col[:, st : st + 1],
-                y_sb[n][:].rearrange("p (u m) -> p u m", u=2),
-                ALU.mult,
+                y_sb[st][:, g * HALF : (g + 1) * HALF].rearrange("p (u m) -> p u m", u=2),
                 ALU.mult,
             )
             da_sb[n] = da
@@ -223,7 +210,7 @@ def tile_moe_bdx_mlp_silu_kernel(
             e, half = divmod(st, 2)
             if half == 0:
                 da_in[e] = work.tile([P, 2, C, 4], BF16, name="da_in", align_bytes=64, bufs=2)
-            da_t = psum.tile([P, 2, 2, P], F32, name="da_t", bufs=1)
+            da_t = psum.tile([P, 2, 2, P], F32, name="da_t", bufs=2)
             for g in range(2):
                 pairs = da_sb[2 * st + g][:].bitcast(F32)
                 for u in range(2):
@@ -258,25 +245,22 @@ def tile_moe_bdx_mlp_silu_kernel(
         nc.tensor.transpose(gate_t[:], gate_rows[:], ident[:])
         gate_col = keep.tile([P, TILES], F32, name="gate_col")
         nc.vector.tensor_scalar_mul(gate_col[:], gate_t[:, 0:TILES], -0.5)
-        tanh_tile(0)
         for k in range(4):
             prepare(0, k)
 
-        for n in range(-3, UNITS + 3):
-            if 0 <= n + 1 < UNITS:
-                derivative(n + 1)
+        for n in range(-5, UNITS + 3):
+            if n % 2 == 0 and 0 <= n + 2 < UNITS:
+                gated_sigmoid((n + 2) // 2)
             if 0 <= n < UNITS:
                 make_da(n)
+            if n % 2 == 1 and 0 <= n + 1 < UNITS:
+                derivative((n + 1) // 2)
             if 0 <= n + 1 < UNITS:
                 product(n + 1)
-            if n + 3 < UNITS:
-                silu_unit(n + 3)
-            if 0 <= n + 2 < UNITS:
-                one_plus_tanh(n + 2)
+            if n + 5 < UNITS:
+                activations(n + 5)
             if n >= 1 and n % 2 == 1 and n // 2 < TILES:
                 turn_da(n // 2)
-            if n % 2 == 0 and 1 <= (n + 4) // 2 < TILES:
-                tanh_tile((n + 4) // 2)
             if n >= 5 and n % 4 == 1:
                 second_product(n // 4 - 1)
             e, k = divmod(n + 1, 4)

@@ -21,9 +21,9 @@ ACT = mybir.ActivationFunctionType
 P = 128
 HALF = 512
 TILES = S // P
-UNITS = 2 * TILES
+STEPS = 2 * E
 GATHER = 512
-V_COLS = 224
+V_COLS = 160
 A_CHUNKS = [(0, 1), (1, 2), (2, 4), (4, 6), (6, 8), (8, 10), (10, 12)]
 
 
@@ -37,6 +37,10 @@ def tile_moe_bdx_mlp_silu_kernel(
         work = ctx.enter_context(tc.tile_pool(name="work", bufs=3))
         psum = ctx.enter_context(tc.psum_pool(name="psum", bufs=2))
 
+        ones = keep.tile([P, P], F32, name="ones")
+        nc.vector.memset(ones[:], 1.0)
+        warm = keep.tile([P, 1], F32, name="warm")
+        nc.scalar.activation(warm[:], ones[:, 0:1], ACT.Silu)
         offs_sb = keep.tile([P, S // 16], U16, name="offs_sb")
         nc.sync.dma_start(offs_sb[:], offs)
         words = keep.tile([P, T], I32, name="words", align_bytes=64)
@@ -56,31 +60,38 @@ def tile_moe_bdx_mlp_silu_kernel(
         def load_a(e):
             for first, last in A_CHUNKS:
                 if first == e:
-                    for u in range(2):
-                        t = load.tile([P, 4, (last - first) * C], F32, name="a_sb", bufs=6)
-                        nc.sync.dma_start(t[:], a_view[u, :, :, first * C : last * C])
-                        for x in range(first, last):
-                            a_sb[x, u] = (t, (x - first) * C)
+                    t = load.tile([P, 2, 4, (last - first) * C], F32, name="a_sb")
+                    width = P if e == 0 else (last - first) * C
+                    for lo in range(0, (last - first) * C, width):
+                        for u in range(2):
+                            nc.sync.dma_start(
+                                t[:, u, :, lo : lo + width], a_view[u, :, :, first * C + lo : first * C + lo + width]
+                            )
+                    for x in range(first, last):
+                        a_sb[x] = (t, (x - first) * C)
+
+        def load_w1(e):
+            raw1 = load.tile([P, 2, 4 * K], F32, name="w1_raw")
+            nc.sync.dma_start(raw1[:], w1[e].rearrange("(g p j) k -> p g (j k)", g=2, j=4))
+            w1_raw[e] = raw1
 
         def load_expert(e):
             raw2 = load.tile([P, 4, H], F32, name="w2_raw")
             src2 = w2[e].rearrange("(p j) h -> p j h", j=4)
-            if e == 0:
-                nc.sync.dma_start(raw2[:, :, 0:HALF], src2[:, :, 0:HALF])
+            if e < 2:
                 load_a(e)
+                nc.sync.dma_start(raw2[:, :, 0:HALF], src2[:, :, 0:HALF])
                 nc.sync.dma_start(raw2[:, :, HALF:H], src2[:, :, HALF:H])
             else:
                 nc.sync.dma_start(raw2[:], src2)
                 load_a(e)
             w2_raw[e] = raw2
-            raw1 = load.tile([P, 2, 4 * K], F32, name="w1_raw")
-            nc.sync.dma_start(raw1[:], w1[e].rearrange("(g p j) k -> p g (j k)", g=2, j=4))
-            w1_raw[e] = raw1
 
         load_expert(0)
         gate_rows = keep.tile([P, P], F32, name="gate_rows")
         nc.sync.dma_start(gate_rows[:], gate.rearrange("h (t p) -> (h t) p", p=P)[0:P, :])
         load_expert(1)
+        load_w1(0)
         pos_sb = []
         for r, pos in enumerate((pos1, pos2, pos3, pos4)):
             t = keep.tile([P, T // 16], U16, name="pos%d" % r)
@@ -90,29 +101,31 @@ def tile_moe_bdx_mlp_silu_kernel(
         g_words, g_scales = {}, {}
 
         def gather_words(c):
-            t = keep.tile([P, GATHER], U32, name="g_words%d" % c, align_bytes=64)
+            t = work.tile([P, GATHER], U32, name="g_words", align_bytes=64, bufs=2)
             cols = slice(c * GATHER // 16, (c + 1) * GATHER // 16)
             nc.vector.tensor_copy(t[:], words[:].bitcast(U32).indirect(offs_sb[:, cols]))
             g_words[c] = t
 
         def gather_scales(c):
-            t = keep.tile([P, GATHER], U8, name="g_scales%d" % c, align_bytes=64)
+            t = work.tile([P, GATHER], U8, name="g_scales", align_bytes=64, bufs=2)
             cols = slice(c * GATHER // 16, (c + 1) * GATHER // 16)
             nc.vector.tensor_copy(t[:], scales[:].indirect(offs_sb[:, cols]))
             g_scales[c] = t
 
         w2_bf, w2_mx, w1_bf, w1_mx = {}, {}, {}, {}
 
-        def cast_w2(e, lo, hi, on_vector):
-            g = lo // HALF
-            if (e, g) not in w2_bf:
-                w2_bf[e, g] = work.tile([P, HALF, 4], BF16, name="w2_bf", align_bytes=64)
-            dst = w2_bf[e, g][:, lo - g * HALF : hi - g * HALF, :].rearrange("p (c i) j -> p c j i", i=4)
-            src = w2_raw[e][:, :, lo:hi].rearrange("p j (c i) -> p c j i", i=4)
-            if on_vector:
-                nc.vector.tensor_copy(dst, src)
-            else:
-                nc.scalar.copy(dst, src)
+        def cast_w2(j):
+            e, g = divmod(j, 2)
+            t = work.tile([P, HALF, 4], BF16, name="w2_bf", align_bytes=64)
+            src = w2_raw[e][:, :, g * HALF : (g + 1) * HALF]
+            split = HALF // 2 if j == 0 else V_COLS * g
+            for copy, lo, hi in ((nc.scalar.copy, split, HALF), (nc.vector.tensor_copy, 0, split)):
+                if hi > lo:
+                    copy(
+                        t[:, lo:hi, :].rearrange("p (c i) j -> p c j i", i=4),
+                        src[:, :, lo:hi].rearrange("p j (c i) -> p c j i", i=4),
+                    )
+            w2_bf[j] = t
 
         def quantise(src, width, name, bufs):
             codes = work.tile([P, width], U32, name=name + "_codes", align_bytes=64, bufs=bufs)
@@ -120,105 +133,120 @@ def tile_moe_bdx_mlp_silu_kernel(
             nc.vector.quantize_mx(out=codes[:].bitcast(FP8X4), scales=plane[:], in_=src)
             return codes, plane
 
-        def quant_w2(e, g):
-            w2_mx[e, g] = quantise(w2_bf[e, g][:].rearrange("p c j -> p (c j)"), HALF, "w2", 4)
+        def quant_w2(j):
+            w2_mx[j] = quantise(w2_bf[j][:].rearrange("p c j -> p (c j)"), HALF, "w2", 3)
 
-        def cast_w1(e, g):
-            if e not in w1_bf:
-                w1_bf[e] = work.tile([P, 2, 4 * K], BF16, name="w1_bf", align_bytes=64, bufs=2)
-            nc.vector.tensor_copy(
-                w1_bf[e][:, g, :].rearrange("p (k u x) -> p k u x", u=2, x=2),
-                w1_raw[e][:, g, :].rearrange("p (x u k) -> p k u x", u=2, x=2),
-            )
+        def cast_w1(e):
+            w1_bf[e] = work.tile([P, 2, 4 * K], BF16, name="w1_bf", align_bytes=64, bufs=2)
+            for g in range(2):
+                nc.vector.tensor_copy(
+                    w1_bf[e][:, g, :].rearrange("p (k u x) -> p k u x", u=2, x=2),
+                    w1_raw[e][:, g, :].rearrange("p (x u k) -> p k u x", u=2, x=2),
+                )
 
         def quant_w1(e):
-            w1_mx[e] = quantise(w1_bf[e][:].rearrange("p g c -> p (g c)"), 2 * K, "w1", 3)
+            w1_mx[e] = quantise(w1_bf[e][:].rearrange("p g c -> p (g c)"), 2 * K, "w1", 2)
 
-        def prepare(e, k):
-            if k == 0:
-                cast_w2(e, V_COLS, HALF, False)
-                cast_w2(e, 0, V_COLS, True)
-            elif k == 1:
-                cast_w2(e, HALF, HALF + 256, False)
-                quant_w2(e, 0)
-            elif k == 2:
-                cast_w2(e, HALF + 256, H, False)
-                cast_w1(e, 0)
-                cast_w1(e, 1)
-            else:
-                quant_w2(e, 1)
-                quant_w1(e)
+        tanh_rows, tanh_sb, silu_sb, t1_ps, prod_ps, y_sb, da_sb, da_in = {}, {}, {}, {}, {}, {}, {}, {}
 
-        tanh_sb, silu_sb, prod_ps, y_sb, da_sb, da_in = {}, {}, {}, {}, {}, {}
+        def a_block(e, half):
+            t, base = a_sb[e]
+            lo = base + half * P
+            return t[:, :, :, lo : lo + P]
 
-        def a_block(st, u):
-            t, base = a_sb[st // 2, u]
-            lo = base + (st % 2) * P
-            return t[:, :, lo : lo + P]
+        def tanh_first(e):
+            t = work.tile([P, 2, 4, P], F32, name="tanh_rows", bufs=2)
+            nc.scalar.activation(t[:], a_block(e, 0), ACT.Tanh, scale=0.5)
+            tanh_rows[e] = t
 
-        def activations(n):
-            st, g = divmod(n, 2)
-            a_t = psum.tile([P, 4, P], F32, name="a_t", bufs=3)
+        def activations(j):
+            e, g = divmod(j, 2)
+            for half in range(2):
+                a_t = psum.tile([P, 4, P], F32, name="a_t", bufs=3)
+                for u in range(2):
+                    for b in range(2):
+                        nc.tensor.transpose(a_t[:, 2 * u + b, :], a_block(e, half)[:, u, 2 * g + b, :], ident[:])
+                flat = a_t[:].rearrange("p b q -> p (b q)")
+                if half == 0:
+                    silu_sb[j, 0] = work.tile([P, HALF], F32, name="silu_first", bufs=4)
+                    nc.scalar.activation(silu_sb[j, 0][:], flat, ACT.Silu, scale=-1.0)
+                else:
+                    if g == 0:
+                        tanh_sb[e] = work.tile([P, H], F32, name="tanh_second", bufs=2)
+                        silu_sb[e, 1] = work.tile([P, H], F32, name="silu_second", bufs=2)
+                    cols = slice(g * HALF, (g + 1) * HALF)
+                    nc.scalar.activation(tanh_sb[e][:, cols], flat, ACT.Tanh, scale=0.5)
+                    nc.scalar.activation(silu_sb[e, 1][:, cols], flat, ACT.Silu, scale=-1.0)
+
+        def one_plus_tanh(j):
+            e, g = divmod(j, 2)
+            t1 = psum.tile([P, 4, P], F32, name="t1", bufs=1)
             for u in range(2):
                 for b in range(2):
-                    nc.tensor.transpose(a_t[:, 2 * u + b, :], a_block(st, u)[:, 2 * g + b, :], ident[:])
-            if g == 0:
-                tanh_sb[st] = work.tile([P, H], F32, name="tanh_sb")
-                silu_sb[st] = work.tile([P, H], F32, name="silu_sb")
-            cols = slice(g * HALF, (g + 1) * HALF)
-            flat = a_t[:].rearrange("p b q -> p (b q)")
-            nc.scalar.activation(tanh_sb[st][:, cols], flat, ACT.Tanh, scale=0.5)
-            nc.scalar.activation(silu_sb[st][:, cols], flat, ACT.Silu, scale=-1.0)
+                    dst = t1[:, 2 * u + b, :]
+                    nc.tensor.matmul(dst, ones[:], ident[:], start=True, stop=False, is_transpose=True)
+                    nc.tensor.matmul(
+                        dst, tanh_rows[e][:, u, 2 * g + b, :], ident[:], start=False, stop=True, is_transpose=True
+                    )
+            t1_ps[j] = t1
 
-        def gated_sigmoid(st):
-            col = gate_col[:, st : st + 1]
-            nc.vector.tensor_scalar(tanh_sb[st][:], tanh_sb[st][:], col, col, ALU.mult, ALU.add)
+        def products(j):
+            codes, plane = w2_mx[j]
+            for half in range(2):
+                c, lo = divmod((j // 2) * C + half * P, GATHER)
+                acc = psum.tile([P, HALF], F32, name="prod")
+                nc.tensor.matmul_mx(
+                    out=acc[:],
+                    lhsT=g_words[c][:, lo : lo + P].bitcast(FP8X4),
+                    lhsT_scale=g_scales[c][:, lo : lo + P],
+                    rhs=codes[:].bitcast(FP8X4),
+                    rhs_scale=plane[:],
+                    start=True,
+                    stop=True,
+                )
+                prod_ps[j, half] = acc
 
-        def product(n):
-            st, g = divmod(n, 2)
-            c, lo = divmod(st * P, GATHER)
-            codes, plane = w2_mx[st // 2, g]
-            acc = psum.tile([P, HALF], F32, name="prod")
-            nc.tensor.matmul_mx(
-                out=acc[:],
-                lhsT=g_words[c][:, lo : lo + P].bitcast(FP8X4),
-                lhsT_scale=g_scales[c][:, lo : lo + P],
-                rhs=codes[:].bitcast(FP8X4),
-                rhs_scale=plane[:],
-                start=True,
-                stop=True,
-            )
-            prod_ps[n] = acc
+        def gated_sigmoid(e):
+            col = gate_col[:, 2 * e + 1 : 2 * e + 2]
+            nc.vector.tensor_scalar(tanh_sb[e][:], tanh_sb[e][:], col, col, ALU.mult, ALU.add)
 
-        def derivative(st):
-            y = work.tile([P, H], F32, name="y_sb", bufs=2)
-            nc.vector.scalar_tensor_tensor(y[:], silu_sb[st][:], 1.0, tanh_sb[st][:], ALU.subtract, ALU.mult)
-            y_sb[st] = y
-
-        def make_da(n):
-            st, g = divmod(n, 2)
-            da = work.tile([P, HALF], BF16, name="da_sb", bufs=4)
-            nc.vector.tensor_tensor(
-                da[:].rearrange("p (u m) -> p u m", u=2),
-                prod_ps[n][:].rearrange("p (m u) -> p u m", u=2),
-                y_sb[st][:, g * HALF : (g + 1) * HALF].rearrange("p (u m) -> p u m", u=2),
-                ALU.mult,
-            )
-            da_sb[n] = da
-
-        def turn_da(st):
-            e, half = divmod(st, 2)
-            if half == 0:
-                da_in[e] = work.tile([P, 2, C, 4], BF16, name="da_in", align_bytes=64, bufs=2)
-            da_t = psum.tile([P, 2, 2, P], F32, name="da_t", bufs=2)
+        def derivative_second(e):
+            y = work.tile([P, H], F32, name="y_second", bufs=2)
+            nc.vector.scalar_tensor_tensor(y[:], silu_sb[e, 1][:], 1.0, tanh_sb[e][:], ALU.subtract, ALU.mult)
             for g in range(2):
-                pairs = da_sb[2 * st + g][:].bitcast(F32)
+                y_sb[2 * e + g, 1] = y[:, g * HALF : (g + 1) * HALF]
+
+        def derivative_first(j):
+            y = work.tile([P, HALF], F32, name="y_first", bufs=2)
+            nc.vector.scalar_tensor_tensor(
+                y[:], silu_sb[j, 0][:], 1.0, t1_ps[j][:].rearrange("p b q -> p (b q)"), ALU.subtract, ALU.mult
+            )
+            y_sb[j, 0] = y[:]
+
+        def make_da(j, half):
+            da = work.tile([P, HALF], BF16, name="da_sb", bufs=4)
+            dst = da[:].rearrange("p (u m) -> p u m", u=2)
+            acc = prod_ps[j, half][:].rearrange("p (m u) -> p u m", u=2)
+            y = y_sb[j, half].rearrange("p (u m) -> p u m", u=2)
+            if half == 0:
+                st = 2 * (j // 2)
+                nc.vector.scalar_tensor_tensor(dst, acc, gate_col[:, st : st + 1], y, ALU.mult, ALU.mult)
+            else:
+                nc.vector.tensor_tensor(dst, acc, y, ALU.mult)
+            da_sb[j, half] = da
+
+        def turn_da(j):
+            e, g = divmod(j, 2)
+            if g == 0:
+                da_in[e] = work.tile([P, 2, C, 4], BF16, name="da_in", align_bytes=64, bufs=2)
+            da_t = psum.tile([P, 2, 2, P], F32, name="da_t", bufs=1)
+            for half in range(2):
+                pairs = da_sb[j, half][:].bitcast(F32)
                 for u in range(2):
-                    nc.tensor.transpose(da_t[:, g, u, :], pairs[:, u * P : (u + 1) * P], ident[:])
-            dst = da_in[e][:].rearrange("p g s t -> p g (s t)").bitcast(F32)
+                    nc.tensor.transpose(da_t[:, half, u, :], pairs[:, u * P : (u + 1) * P], ident[:])
+            dst = da_in[e][:, g, :, :].rearrange("p s t -> p (s t)").bitcast(F32)
             nc.scalar.copy(
-                dst[:, :, half * 2 * P : (half + 1) * 2 * P].rearrange("p g (s u) -> p g s u", u=2),
-                da_t[:].rearrange("p g u s -> p g s u"),
+                dst.rearrange("p (h s u) -> p h s u", h=2, u=2), da_t[:].rearrange("p h u s -> p h s u")
             )
 
         dx_all = keep.tile([P, S], F32, name="dx_all")
@@ -245,40 +273,56 @@ def tile_moe_bdx_mlp_silu_kernel(
         nc.tensor.transpose(gate_t[:], gate_rows[:], ident[:])
         gate_col = keep.tile([P, TILES], F32, name="gate_col")
         nc.vector.tensor_scalar_mul(gate_col[:], gate_t[:, 0:TILES], -0.5)
-        for k in range(4):
-            prepare(0, k)
 
-        for n in range(-5, UNITS + 3):
-            if n % 2 == 0 and 0 <= n + 2 < UNITS:
-                gated_sigmoid((n + 2) // 2)
-            if 0 <= n < UNITS:
-                make_da(n)
-            if n % 2 == 1 and 0 <= n + 1 < UNITS:
-                derivative((n + 1) // 2)
-            if 0 <= n + 1 < UNITS:
-                product(n + 1)
-            if n + 5 < UNITS:
-                activations(n + 5)
-            if n >= 1 and n % 2 == 1 and n // 2 < TILES:
-                turn_da(n // 2)
-            if n >= 5 and n % 4 == 1:
-                second_product(n // 4 - 1)
-            e, k = divmod(n + 1, 4)
-            if 0 <= e and e + 1 < E:
-                if k == 0 and e + 2 < E:
-                    load_expert(e + 2)
-                prepare(e + 1, k)
-                if e % 2 == 1 and k == 0:
-                    gather_words((e + 1) // 2)
-                if e % 2 == 1 and k == 2:
-                    gather_scales((e + 1) // 2)
+        for j in range(-3, STEPS + 2):
+            e, g = divmod(j, 2)
+            live = 0 <= j < STEPS
+            if live and g == 0 and e + 2 < E:
+                load_expert(e + 2)
+            if live and g == 0 and e + 1 < E:
+                load_w1(e + 1)
+            if g == 1 and e >= 1:
+                second_product(e - 1)
+            if g == 1 and 0 <= e + 1 < E:
+                gated_sigmoid(e + 1)
+            if g == 0 and e >= 1:
+                quant_w1(e - 1)
+            if live and j % 4 == 0 and j + 4 < STEPS:
+                gather_words(j // 4 + 1)
+            if live and j % 4 == 2 and j + 2 < STEPS:
+                gather_scales(j // 4 + 1)
+            if 0 <= j + 1 < STEPS:
+                quant_w2(j + 1)
+            if live and g == 0:
+                derivative_second(e)
+            if 0 <= j + 2 < STEPS:
+                cast_w2(j + 2)
+            if live:
+                make_da(j, 0)
+            if live and g == 0:
+                cast_w1(e)
+            if live:
+                make_da(j, 1)
+            if 0 <= j + 1 < STEPS:
+                derivative_first(j + 1)
+            if 0 <= j + 1 < STEPS:
+                products(j + 1)
+            if g == 1 and j + 3 < STEPS:
+                tanh_first((j + 3) // 2)
+            if 0 <= j + 2 < STEPS:
+                one_plus_tanh(j + 2)
+            if live:
+                turn_da(j)
+            if j + 3 < STEPS:
+                activations(j + 3)
 
-        picked = [keep.tile([P, T], F32, name="picked%d" % r) for r in range(4)]
+        picked_all = load.tile([P, 4, T], F32, name="w2_raw")
+        picked = [picked_all[:, r, :] for r in range(4)]
         for r in range(3):
-            nc.vector.tensor_copy(picked[r][:], dx_all[:].indirect(pos_sb[r][:]))
-        nc.vector.tensor_add(picked[0][:], picked[0][:], picked[1][:])
-        nc.vector.tensor_copy(picked[3][:], dx_all[:].indirect(pos_sb[3][:]))
-        nc.vector.tensor_add(picked[0][:], picked[0][:], picked[2][:])
+            nc.vector.tensor_copy(picked[r], dx_all[:].indirect(pos_sb[r][:]))
+        nc.vector.tensor_add(picked[0], picked[0], picked[1])
+        nc.vector.tensor_copy(picked[3], dx_all[:].indirect(pos_sb[3][:]))
+        nc.vector.tensor_add(picked[0], picked[0], picked[2])
         for h in range(2):
             cols = slice(h * T // 2, (h + 1) * T // 2)
             nc.vector.tensor_add(picked[0][:, cols], picked[0][:, cols], picked[3][:, cols])

from contextlib import ExitStack

import concourse.mybir as mybir
from concourse.masks import make_identity

K, T, E, C, H, N = 128, 768, 12, 256, 1024, 512
S = E * C
FLOPS = 2 * S * H * (N + K)
BYTES = 4 * (E * N * H + E * H * K + H * S + S + K * T) + 128 * T * 4 + 16 * T + 128 * 2 * (S + 4 * T) // 16

F32 = mybir.dt.float32
BF16 = mybir.dt.bfloat16
I32 = mybir.dt.int32
U32 = mybir.dt.uint32
U16 = mybir.dt.uint16
U8 = mybir.dt.uint8
FP8X4 = mybir.dt.float8_e4m3fn_x4
ALU = mybir.AluOpType
ACT = mybir.ActivationFunctionType

P = 128
HALF = 512
TILES = S // P
STEPS = 2 * E
GATHER = 512
V_COLS = 160
A_CHUNKS = [(0, 1), (1, 2), (2, 4), (4, 6), (6, 8), (8, 10), (10, 12)]


def tile_moe_bdx_mlp_silu_kernel(
    tc, dy_words, dy_scales, a, w2, w1, gate, offs, pos1, pos2, pos3, pos4, out
):
    nc = tc.nc
    with ExitStack() as ctx:
        keep = ctx.enter_context(tc.tile_pool(name="keep", bufs=1))
        load = ctx.enter_context(tc.tile_pool(name="load", bufs=3))
        work = ctx.enter_context(tc.tile_pool(name="work", bufs=3))
        psum = ctx.enter_context(tc.psum_pool(name="psum", bufs=2))

        ones = keep.tile([P, P], F32, name="ones")
        nc.vector.memset(ones[:], 1.0)
        warm = keep.tile([P, 1], F32, name="warm")
        nc.scalar.activation(warm[:], ones[:, 0:1], ACT.Silu)
        offs_sb = keep.tile([P, S // 16], U16, name="offs_sb")
        nc.sync.dma_start(offs_sb[:], offs)
        words = keep.tile([P, T], I32, name="words", align_bytes=64)
        nc.sync.dma_start(words[:], dy_words[0].rearrange("p t d -> p (t d)").bitcast(I32))
        scales = keep.tile([P, T], U8, name="scales", align_bytes=64)
        nc.gpsimd.memset(scales[:], 0)
        for q in range(4):
            nc.scalar.dma_start(
                scales[32 * q : 32 * q + 4, :].bitcast(I32), dy_scales[0, 4 * q : 4 * q + 4, :].bitcast(I32)
            )
        ident = keep.tile([P, P], F32, name="ident")
        make_identity(nc, ident[:])

        a_view = a.rearrange("(b q u) s -> u q b s", q=P, u=2)
        a_sb, w2_raw, w1_raw = {}, {}, {}

        def load_a(e):
            for first, last in A_CHUNKS:
                if first == e:
                    t = load.tile([P, 2, 4, (last - first) * C], F32, name="a_sb")
                    width = P if e == 0 else (last - first) * C
                    for lo in range(0, (last - first) * C, width):
                        for u in range(2):
                            nc.sync.dma_start(
                                t[:, u, :, lo : lo + width], a_view[u, :, :, first * C + lo : first * C + lo + width]
                            )
                    for x in range(first, last):
                        a_sb[x] = (t, (x - first) * C)

        def load_w1(e):
            raw1 = load.tile([P, 2, 4 * K], F32, name="w1_raw")
            nc.sync.dma_start(raw1[:], w1[e].rearrange("(g p j) k -> p g (j k)", g=2, j=4))
            w1_raw[e] = raw1

        def load_expert(e):
            raw2 = load.tile([P, 4, H], F32, name="w2_raw")
            src2 = w2[e].rearrange("(p j) h -> p j h", j=4)
            if e < 2:
                load_a(e)
                nc.sync.dma_start(raw2[:, :, 0:HALF], src2[:, :, 0:HALF])
                nc.sync.dma_start(raw2[:, :, HALF:H], src2[:, :, HALF:H])
            else:
                nc.sync.dma_start(raw2[:], src2)
                load_a(e)
            w2_raw[e] = raw2

        load_expert(0)
        gate_rows = keep.tile([P, P], F32, name="gate_rows")
        nc.sync.dma_start(gate_rows[:], gate.rearrange("h (t p) -> (h t) p", p=P)[0:P, :])
        load_expert(1)
        load_w1(0)
        pos_sb = []
        for r, pos in enumerate((pos1, pos2, pos3, pos4)):
            t = keep.tile([P, T // 16], U16, name="pos%d" % r)
            nc.sync.dma_start(t[:], pos)
            pos_sb.append(t)

        g_words, g_scales = {}, {}

        def gather_words(c):
            t = work.tile([P, GATHER], U32, name="g_words", align_bytes=64, bufs=2)
            cols = slice(c * GATHER // 16, (c + 1) * GATHER // 16)
            nc.vector.tensor_copy(t[:], words[:].bitcast(U32).indirect(offs_sb[:, cols]))
            g_words[c] = t

        def gather_scales(c):
            t = work.tile([P, GATHER], U8, name="g_scales", align_bytes=64, bufs=2)
            cols = slice(c * GATHER // 16, (c + 1) * GATHER // 16)
            nc.vector.tensor_copy(t[:], scales[:].indirect(offs_sb[:, cols]))
            g_scales[c] = t

        w2_bf, w2_mx, w1_bf, w1_mx = {}, {}, {}, {}

        def cast_w2(j):
            e, g = divmod(j, 2)
            t = work.tile([P, HALF, 4], BF16, name="w2_bf", align_bytes=64)
            src = w2_raw[e][:, :, g * HALF : (g + 1) * HALF]
            split = HALF // 2 if j == 0 else V_COLS * g
            for copy, lo, hi in ((nc.scalar.copy, split, HALF), (nc.vector.tensor_copy, 0, split)):
                if hi > lo:
                    copy(
                        t[:, lo:hi, :].rearrange("p (c i) j -> p c j i", i=4),
                        src[:, :, lo:hi].rearrange("p j (c i) -> p c j i", i=4),
                    )
            w2_bf[j] = t

        def quantise(src, width, name, bufs):
            codes = work.tile([P, width], U32, name=name + "_codes", align_bytes=64, bufs=bufs)
            plane = work.tile([P, width], U8, name=name + "_plane", align_bytes=64, bufs=bufs)
            nc.vector.quantize_mx(out=codes[:].bitcast(FP8X4), scales=plane[:], in_=src)
            return codes, plane

        def quant_w2(j):
            w2_mx[j] = quantise(w2_bf[j][:].rearrange("p c j -> p (c j)"), HALF, "w2", 3)

        def cast_w1(e):
            w1_bf[e] = work.tile([P, 2, 4 * K], BF16, name="w1_bf", align_bytes=64, bufs=2)
            for g in range(2):
                nc.vector.tensor_copy(
                    w1_bf[e][:, g, :].rearrange("p (k u x) -> p k u x", u=2, x=2),
                    w1_raw[e][:, g, :].rearrange("p (x u k) -> p k u x", u=2, x=2),
                )

        def quant_w1(e):
            w1_mx[e] = quantise(w1_bf[e][:].rearrange("p g c -> p (g c)"), 2 * K, "w1", 2)

        tanh_rows, tanh_sb, silu_sb, t1_ps, prod_ps, y_sb, da_sb, da_in = {}, {}, {}, {}, {}, {}, {}, {}

        def a_block(e, half):
            t, base = a_sb[e]
            lo = base + half * P
            return t[:, :, :, lo : lo + P]

        def tanh_first(e):
            t = work.tile([P, 2, 4, P], F32, name="tanh_rows", bufs=2)
            nc.scalar.activation(t[:], a_block(e, 0), ACT.Tanh, scale=0.5)
            tanh_rows[e] = t

        def activations(j):
            e, g = divmod(j, 2)
            for half in range(2):
                a_t = psum.tile([P, 4, P], F32, name="a_t", bufs=3)
                for u in range(2):
                    for b in range(2):
                        nc.tensor.transpose(a_t[:, 2 * u + b, :], a_block(e, half)[:, u, 2 * g + b, :], ident[:])
                flat = a_t[:].rearrange("p b q -> p (b q)")
                if half == 0:
                    silu_sb[j, 0] = work.tile([P, HALF], F32, name="silu_first", bufs=4)
                    nc.scalar.activation(silu_sb[j, 0][:], flat, ACT.Silu, scale=-1.0)
                else:
                    if g == 0:
                        tanh_sb[e] = work.tile([P, H], F32, name="tanh_second", bufs=2)
                        silu_sb[e, 1] = work.tile([P, H], F32, name="silu_second", bufs=2)
                    cols = slice(g * HALF, (g + 1) * HALF)
                    nc.scalar.activation(tanh_sb[e][:, cols], flat, ACT.Tanh, scale=0.5)
                    nc.scalar.activation(silu_sb[e, 1][:, cols], flat, ACT.Silu, scale=-1.0)

        def one_plus_tanh(j):
            e, g = divmod(j, 2)
            t1 = psum.tile([P, 4, P], F32, name="t1", bufs=1)
            for u in range(2):
                for b in range(2):
                    dst = t1[:, 2 * u + b, :]
                    nc.tensor.matmul(dst, ones[:], ident[:], start=True, stop=False, is_transpose=True)
                    nc.tensor.matmul(
                        dst, tanh_rows[e][:, u, 2 * g + b, :], ident[:], start=False, stop=True, is_transpose=True
                    )
            t1_ps[j] = t1

        def products(j):
            codes, plane = w2_mx[j]
            for half in range(2):
                c, lo = divmod((j // 2) * C + half * P, GATHER)
                acc = psum.tile([P, HALF], F32, name="prod")
                nc.tensor.matmul_mx(
                    out=acc[:],
                    lhsT=g_words[c][:, lo : lo + P].bitcast(FP8X4),
                    lhsT_scale=g_scales[c][:, lo : lo + P],
                    rhs=codes[:].bitcast(FP8X4),
                    rhs_scale=plane[:],
                    start=True,
                    stop=True,
                )
                prod_ps[j, half] = acc

        def gated_sigmoid(e):
            col = gate_col[:, 2 * e + 1 : 2 * e + 2]
            nc.vector.tensor_scalar(tanh_sb[e][:], tanh_sb[e][:], col, col, ALU.mult, ALU.add)

        def derivative_second(e):
            y = work.tile([P, H], F32, name="y_second", bufs=2)
            nc.vector.scalar_tensor_tensor(y[:], silu_sb[e, 1][:], 1.0, tanh_sb[e][:], ALU.subtract, ALU.mult)
            for g in range(2):
                y_sb[2 * e + g, 1] = y[:, g * HALF : (g + 1) * HALF]

        def derivative_first(j):
            y = work.tile([P, HALF], F32, name="y_first", bufs=2)
            nc.vector.scalar_tensor_tensor(
                y[:], silu_sb[j, 0][:], 1.0, t1_ps[j][:].rearrange("p b q -> p (b q)"), ALU.subtract, ALU.mult
            )
            y_sb[j, 0] = y[:]

        def make_da(j, half):
            da = work.tile([P, HALF], BF16, name="da_sb", bufs=4)
            dst = da[:].rearrange("p (u m) -> p u m", u=2)
            acc = prod_ps[j, half][:].rearrange("p (m u) -> p u m", u=2)
            y = y_sb[j, half].rearrange("p (u m) -> p u m", u=2)
            if half == 0:
                st = 2 * (j // 2)
                nc.vector.scalar_tensor_tensor(dst, acc, gate_col[:, st : st + 1], y, ALU.mult, ALU.mult)
            else:
                nc.vector.tensor_tensor(dst, acc, y, ALU.mult)
            da_sb[j, half] = da

        def turn_da(j):
            e, g = divmod(j, 2)
            if g == 0:
                da_in[e] = work.tile([P, 2, C, 4], BF16, name="da_in", align_bytes=64, bufs=2)
            da_t = psum.tile([P, 2, 2, P], F32, name="da_t", bufs=1)
            for half in range(2):
                pairs = da_sb[j, half][:].bitcast(F32)
                for u in range(2):
                    nc.tensor.transpose(da_t[:, half, u, :], pairs[:, u * P : (u + 1) * P], ident[:])
            dst = da_in[e][:, g, :, :].rearrange("p s t -> p (s t)").bitcast(F32)
            nc.scalar.copy(
                dst.rearrange("p (h s u) -> p h s u", h=2, u=2), da_t[:].rearrange("p h u s -> p h s u")
            )

        dx_all = keep.tile([P, S], F32, name="dx_all")

        def second_product(e):
            codes, plane = quantise(da_in[e][:].rearrange("p g s t -> p (g s t)"), 2 * C, "da", 2)
            w_codes, w_plane = w1_mx[e]
            acc = psum.tile([P, C], F32, name="dx", bufs=1)
            for g in range(2):
                nc.tensor.matmul_mx(
                    out=acc[:],
                    lhsT=w_codes[:, g * K : (g + 1) * K].bitcast(FP8X4),
                    lhsT_scale=w_plane[:, g * K : (g + 1) * K],
                    rhs=codes[:, g * C : (g + 1) * C].bitcast(FP8X4),
                    rhs_scale=plane[:, g * C : (g + 1) * C],
                    start=(g == 0),
                    stop=(g == 1),
                )
            nc.scalar.copy(dx_all[:, e * C : (e + 1) * C], acc[:])

        gather_words(0)
        gather_scales(0)
        gate_t = psum.tile([P, P], F32, name="dx", bufs=1)
        nc.tensor.transpose(gate_t[:], gate_rows[:], ident[:])
        gate_col = keep.tile([P, TILES], F32, name="gate_col")
        nc.vector.tensor_scalar_mul(gate_col[:], gate_t[:, 0:TILES], -0.5)

        for j in range(-3, STEPS + 2):
            e, g = divmod(j, 2)
            live = 0 <= j < STEPS
            if live and g == 0 and e + 2 < E:
                load_expert(e + 2)
            if live and g == 0 and e + 1 < E:
                load_w1(e + 1)
            if g == 1 and e >= 1:
                second_product(e - 1)
            if g == 1 and 0 <= e + 1 < E:
                gated_sigmoid(e + 1)
            if g == 0 and e >= 1:
                quant_w1(e - 1)
            if live and j % 4 == 0 and j + 4 < STEPS:
                gather_words(j // 4 + 1)
            if live and j % 4 == 2 and j + 2 < STEPS:
                gather_scales(j // 4 + 1)
            if 0 <= j + 1 < STEPS:
                quant_w2(j + 1)
            if live and g == 0:
                derivative_second(e)
            if 0 <= j + 2 < STEPS:
                cast_w2(j + 2)
            if live:
                make_da(j, 0)
            if live and g == 0:
                cast_w1(e)
            if live:
                make_da(j, 1)
            if 0 <= j + 1 < STEPS:
                derivative_first(j + 1)
            if 0 <= j + 1 < STEPS:
                products(j + 1)
            if g == 1 and j + 3 < STEPS:
                tanh_first((j + 3) // 2)
            if 0 <= j + 2 < STEPS:
                one_plus_tanh(j + 2)
            if live:
                turn_da(j)
            if j + 3 < STEPS:
                activations(j + 3)

        picked_all = load.tile([P, 4, T], F32, name="w2_raw")
        picked = [picked_all[:, r, :] for r in range(4)]
        for r in range(3):
            nc.vector.tensor_copy(picked[r], dx_all[:].indirect(pos_sb[r][:]))
        nc.vector.tensor_add(picked[0], picked[0], picked[1])
        nc.vector.tensor_copy(picked[3], dx_all[:].indirect(pos_sb[3][:]))
        nc.vector.tensor_add(picked[0], picked[0], picked[2])
        for h in range(2):
            cols = slice(h * T // 2, (h + 1) * T // 2)
            nc.vector.tensor_add(picked[0][:, cols], picked[0][:, cols], picked[3][:, cols])
            nc.sync.dma_start(out[:, cols], picked[0][:, cols])
